import numpy as np
import ml_dtypes


def mxq(x, axis, fmt="e4m3"):
    dtype, down = {"e4m3": (ml_dtypes.float8_e4m3fn, 7), "e5m2": (ml_dtypes.float8_e5m2, 14)}[fmt]
    v = np.moveaxis(np.asarray(x, np.float32).astype(ml_dtypes.bfloat16).astype(np.float64), axis, -1)
    blocks = v.reshape(v.shape[:-1] + (-1, 32))
    amax = np.abs(blocks).max(-1, keepdims=True)
    byte = np.maximum(np.where(amax > 0, np.frexp(amax)[1] - 1 + 127, 0) - down, 1)
    scale = np.exp2(byte - 127.0)
    codes = (blocks / scale).astype(np.float32).astype(dtype).astype(np.float64)
    return np.moveaxis((codes * scale).reshape(v.shape), -1, axis)


WIDE = False


def mx_kscale(k):
    if not WIDE:
        return np.ones(k)
    levels = np.array([10, -10, 5, -5, 0])
    if k % 512:
        return np.exp2(np.random.permutation(np.resize(levels, k // 32))).repeat(32)
    a = np.empty((k // 512, 16))
    for p in range(k // 512):
        a[p, :8] = np.random.permutation(np.resize(levels, 8))
        for g in range(8):
            far = levels[np.abs(levels - a[p, g]) >= 10]
            a[p, g + 8] = far[np.random.randint(len(far))]
    return np.exp2(a.ravel()).repeat(32)


def f64(x):
    return np.asarray(x).astype(np.float64)


def striped(idx):
    return np.tile(idx.reshape(-1, 16).T, (8, 1)).astype(np.uint16)


def unstriped(offs):
    return offs[:16].T.reshape(-1).astype(np.int64)


def pack_weight(w):
    k, n = w.shape
    w = f64(np.asarray(w, np.float32).astype(ml_dtypes.bfloat16)).reshape(k // 32, 32, n)
    amax = np.abs(w).max(1)
    byte = np.clip(np.where(amax > 0, np.frexp(amax)[1] - 1 + 127 - 7, 1), 1, 254)
    scaled = (w * np.exp2(127.0 - byte)[:, None, :]).reshape(k, n).astype(np.float32)
    words = np.ascontiguousarray(scaled.reshape(k // 512, 128, 4, n).transpose(0, 1, 3, 2)).astype(ml_dtypes.float8_e4m3fn).view(np.uint8)
    return words, np.ascontiguousarray(byte.astype(np.uint8).reshape(k // 512, 16, n))


def unpack_weight(words, scales):
    g, p, n, _ = words.shape
    vals = np.ascontiguousarray(words).view(ml_dtypes.float8_e4m3fn).astype(np.float64) * np.repeat(np.exp2(scales.astype(np.float64) - 127.0), 8, axis=1)[..., None]
    return vals.transpose(0, 1, 3, 2).reshape(g * 512, n)


def sigmoid(v):
    return 1.0 / (1.0 + np.exp(-np.maximum(v, -700.0)))


K, T, S, D, N, V = 512, 2048, 512, 4, 256, 128
P = 2 ** 7


def setup_inputs():
    n = np.random.standard_normal
    s = mx_kscale(K)[:, None]
    packed_xT = pack_weight(n((K, T)) * s)
    return {
        "x_words": packed_xT[0],
        "x_scales": packed_xT[1],
        "w1": (n((K, N)) / np.sqrt(K) / s).astype(np.float32),
        "w2": (n((K, N)) / np.sqrt(K) / s).astype(np.float32),
        "px": (n((N, V))).astype(np.float32),
        "py": (n((N, V))).astype(np.float32),
        "bx": (np.tile(n(S), (P, 1))).astype(np.float32),
        "by": (np.tile(n(S), (P, 1))).astype(np.float32),
        "il": (np.tile(np.random.uniform(0.5, 1.5, S), (P, 1))).astype(np.float32),
        "crit": (-np.random.uniform(1.0, 2.5, (N, 1))).astype(np.float32),
        "vol": (np.tile(np.random.uniform(0.5, 1.5, S), (P, 1))).astype(np.float32),
        "offs": striped(np.random.permutation(T)[:S]),
    }


def reference(x_words, x_scales, w1, w2, px, py, bx, by, il, crit, vol, offs):
    xq = unpack_weight(x_words, x_scales)[:, unstriped(offs)]
    y = mxq(f64(w1), 0, "e4m3").T @ xq
    dx = y - (np.repeat(f64(px), D, axis=1)) + f64(bx)[:1]
    z = mxq(f64(w2), 0, "e4m3").T @ xq
    dy = z - (np.repeat(f64(py), D, axis=1)) + f64(by)[:1]
    ln = np.sqrt((dx) ** 2 + (dy) ** 2 + 0.05)
    stc = ln * f64(il)[:1]
    mu = sigmoid(-4.0 * (stc + f64(crit)))
    mv = mu * f64(vol)[:1]
    return -1.0 * ((mv.reshape(len(mv), -1, D).sum(axis=2)) / (f64(vol)[:1].reshape(len(f64(vol)[:1]), -1, D).sum(axis=2))) + 1.0

@@ -1,0 +1,173 @@
+from contextlib import ExitStack
+
+import concourse.mybir as mybir
+from concourse.masks import make_identity
+
+K, T, S, D, N, V = 512, 2048, 512, 4, 256, 128
+P = 128
+PACK = 4
+M_TILES = N // P
+SCALE_ROWS = 4
+QUADRANTS = 4
+
+FLOPS = 2 * 2 * K * N * S
+BYTES = K * T + (K // 32) * T + 4 * (2 * K * N + 3 * N * V + 4 * S + N) + 2 * P * (S // 16)
+
+F32 = mybir.dt.float32
+BF16 = mybir.dt.bfloat16
+I32 = mybir.dt.int32
+U32 = mybir.dt.uint32
+U16 = mybir.dt.uint16
+U8 = mybir.dt.uint8
+FP8X4 = mybir.dt.float8_e4m3fn_x4
+ACT = mybir.ActivationFunctionType
+ALU = mybir.AluOpType
+AXIS = mybir.AxisListType
+
+SCALAR_COLS = 128
+
+
+def tile_picked_yperid_dmg_p_kernel(
+    tc, x_words, x_scales, w1, w2, px, py, bx, by, il, crit, vol, offs, out
+):
+    nc = tc.nc
+    with ExitStack() as ctx:
+        keep = ctx.enter_context(tc.tile_pool(name="keep", bufs=1))
+        psum = ctx.enter_context(tc.psum_pool(name="psum", bufs=1))
+
+        def bank(b, cols):
+            return psum.tile([P, cols], F32, name=f"bank{b}", tag=f"bank{b}")
+
+        offsets = keep.tile([P, S // 16], U16)
+        nc.sync.dma_start(offsets[:], offs)
+
+        table_scales = keep.tile([P, T], U8)
+        nc.vector.memset(table_scales[:].bitcast(I32), 0)
+        one_in = keep.tile([P, 1], F32)
+        nc.vector.memset(one_in[:], 1.0)
+        one = keep.tile([P, 1], F32)
+        nc.scalar.activation(one[:], one_in[:], ACT.Sqrt)
+
+        ident = keep.tile([P, P], F32)
+        make_identity(nc, ident[:])
+
+        point = []
+        for name, src in (("px_rows", px), ("py_rows", py)):
+            rows = keep.tile([P, M_TILES, V], F32, name=name)
+            nc.sync.dma_start(rows[:], src.rearrange("(t p) v -> p t v", p=P))
+            point.append(rows)
+
+        for q in range(QUADRANTS):
+            nc.sync.dma_start(
+                table_scales[32 * q : 32 * q + SCALE_ROWS, :].bitcast(I32),
+                x_scales[0, SCALE_ROWS * q : SCALE_ROWS * (q + 1), :].bitcast(I32),
+            )
+        table_words = keep.tile([P, T], I32)
+        nc.sync.dma_start(table_words[:], x_words[0].rearrange("p c r -> p (c r)").bitcast(I32))
+
+        w_raw = []
+        for name, src in (("w1_raw", w1), ("w2_raw", w2)):
+            raw = keep.tile([P, PACK, N], F32, name=name)
+            nc.sync.dma_start(raw[:], src.rearrange("(p j) m -> p j m", j=PACK))
+            w_raw.append(raw)
+
+        def load_bond_row(name, src):
+            cols = keep.tile([P, D], F32, name=name)
+            nc.gpsimd.dma_start(cols[:], src[0].rearrange("(v d) -> v d", d=D))
+            return cols
+
+        bond = [load_bond_row("bx_cols", bx), load_bond_row("by_cols", by)]
+        crit_cols = keep.tile([P, M_TILES], F32)
+        with nc.allow_non_contiguous_dma(reason="one value a partition"):
+            nc.gpsimd.dma_start(crit_cols[:], crit.rearrange("(t p) o -> p (t o)", p=P))
+        il_cols = load_bond_row("il_cols", il)
+        vol_cols = load_bond_row("vol_cols", vol)
+
+        picked_scales = keep.tile([P, S], U8)
+        nc.vector.tensor_copy(picked_scales[:], table_scales[:].indirect(offsets[:]))
+        x_scale = keep.tile([P, D, V], U8, align_bytes=64)
+        nc.vector.tensor_copy(x_scale[:], picked_scales[:].rearrange("p (v d) -> p d v", d=D))
+        x_codes = keep.tile([P, D, V], U32, align_bytes=64)
+        nc.vector.tensor_copy(
+            x_codes[:].rearrange("p d v -> p v d"), table_words[:].bitcast(U32).indirect(offsets[:])
+        )
+
+        point_ps = bank(6, 2 * N)
+        for c in range(2):
+            for t in range(M_TILES):
+                nc.tensor.transpose(point_ps[:, c * N + t * P : c * N + (t + 1) * P], point[c][:, t, :], ident[:])
+        point_t = keep.tile([P, 2 * N], F32)
+        nc.scalar.copy(point_t[:], point_ps[:])
+
+        crit_ps = bank(7, N)
+        for t in range(M_TILES):
+            nc.tensor.transpose(crit_ps[:, t * P : (t + 1) * P], crit_cols[:, t : t + 1].to_broadcast([P, P]), ident[:])
+        crit_t = keep.tile([P, N], F32)
+        nc.scalar.copy(crit_t[:], crit_ps[:])
+
+        squares = []
+        for c in range(2):
+            grouped = keep.tile([P, N, PACK], BF16, name=f"grouped{c}", align_bytes=64)
+            dst = grouped[:].rearrange("p (g i) j -> p g j i", i=4)
+            src = w_raw[c][:].rearrange("p j (g i) -> p g j i", i=4)
+            cut = SCALAR_COLS // 4
+            nc.scalar.copy(dst[:, :cut], src[:, :cut])
+            nc.vector.tensor_copy(dst[:, cut:], src[:, cut:])
+            codes = keep.tile([P, N], U32, name=f"w_codes{c}", align_bytes=64)
+            scales = keep.tile([P, N], U8, name=f"w_scales{c}", align_bytes=64)
+            nc.vector.quantize_mx(
+                out=codes[:].bitcast(FP8X4), scales=scales[:], in_=grouped[:].rearrange("p m j -> p (m j)")
+            )
+            diff = keep.tile([P, D, N], F32, name=f"diff{c}")
+            square = keep.tile([P, D, N], F32, name=f"square{c}")
+            for d in range(D):
+                acc = bank(D * c + d, N)
+                nc.tensor.matmul_mx(
+                    out=acc[:],
+                    lhsT=x_codes[:, d, :].bitcast(FP8X4),
+                    lhsT_scale=x_scale[:, d, :],
+                    rhs=codes[:].bitcast(FP8X4),
+                    rhs_scale=scales[:],
+                    start=True,
+                    stop=True,
+                )
+                nc.vector.scalar_tensor_tensor(
+                    diff[:, d, :], acc[:], bond[c][:, d : d + 1], point_t[:, c * N : (c + 1) * N], ALU.add, ALU.subtract
+                )
+                nc.scalar.activation(square[:, d, :], diff[:, d, :], ACT.Square)
+            squares.append(square)
+
+        length2 = keep.tile([P, D, N], F32, tag="staged")
+        length = keep.tile([P, D, N], F32)
+        margin = keep.tile([P, D, N], F32)
+        for d in range(D):
+            nc.vector.scalar_tensor_tensor(
+                length2[:, d, :], squares[0][:, d, :], 0.05, squares[1][:, d, :], ALU.add, ALU.add
+            )
+            nc.scalar.activation(length[:, d, :], length2[:, d, :], ACT.Sqrt)
+        for d in range(D):
+            nc.vector.scalar_tensor_tensor(
+                margin[:, d, :], length[:, d, :], il_cols[:, d : d + 1], crit_t[:], ALU.mult, ALU.add
+            )
+
+        vol_sum = keep.tile([P, 1], F32)
+        nc.vector.tensor_reduce(vol_sum[:], vol_cols[:], AXIS.X, ALU.add)
+        vol_inv = keep.tile([P, 1], F32)
+        nc.vector.reciprocal(vol_inv[:], vol_sum[:])
+        share = keep.tile([P, D], F32)
+        nc.vector.tensor_scalar(share[:], vol_cols[:], vol_inv[:], -1.0, ALU.mult, ALU.mult)
+
+        intact = keep.tile([P, D, N], F32, tag="staged")
+        weighted = keep.tile([P, D, N], F32)
+        for t in range(M_TILES):
+            cols = slice(t * P, (t + 1) * P)
+            total = bank(t, V)
+            for d in range(D):
+                nc.scalar.activation(intact[:, d, cols], margin[:, d, cols], ACT.Sigmoid, scale=-4.0)
+                nc.vector.tensor_scalar(weighted[:, d, cols], intact[:, d, cols], share[:, d : d + 1], None, ALU.mult)
+                nc.tensor.matmul(
+                    total[:], weighted[:, d, cols], ident[:], start=(d == 0), stop=(d == D - 1), is_transpose=True
+                )
+            result = keep.tile([P, V], F32, name=f"result{t}")
+            nc.vector.tensor_scalar(result[:], total[:], one[:], None, ALU.add)
+            nc.sync.dma_start(out[cols, :], result[:])

@@ -24,7 +24,7 @@ ACT = mybir.ActivationFunctionType
 ALU = mybir.AluOpType
 AXIS = mybir.AxisListType
 
-SCALAR_COLS = 128
+W2_SCALAR_COLS = 128
 
 
 def tile_picked_yperid_dmg_p_kernel(
@@ -38,51 +38,76 @@ def tile_picked_yperid_dmg_p_kernel(
         def bank(b, cols):
             return psum.tile([P, cols], F32, name=f"bank{b}", tag=f"bank{b}")
 
-        offsets = keep.tile([P, S // 16], U16)
-        nc.sync.dma_start(offsets[:], offs)
+        def load_bond_row(name, src):
+            cols = keep.tile([P, D], F32, name=name)
+            nc.sync.dma_start(cols[:], src[0].rearrange("(v d) -> v d", d=D))
+            return cols
+
+        def load_points(name, src):
+            rows = keep.tile([P, M_TILES, V], F32, name=name)
+            nc.sync.dma_start(rows[:], src.rearrange("(t p) v -> p t v", p=P))
+            return rows
+
+        def load_weights(name, src):
+            raw = keep.tile([P, PACK, N], F32, name=name)
+            nc.sync.dma_start(raw[:], src.rearrange("(p j) m -> p j m", j=PACK))
+            return raw
 
         table_scales = keep.tile([P, T], U8)
-        nc.vector.memset(table_scales[:].bitcast(I32), 0)
+        nc.gpsimd.memset(table_scales[:].bitcast(I32), 0)
         one_in = keep.tile([P, 1], F32)
         nc.vector.memset(one_in[:], 1.0)
         one = keep.tile([P, 1], F32)
         nc.scalar.activation(one[:], one_in[:], ACT.Sqrt)
-
         ident = keep.tile([P, P], F32)
         make_identity(nc, ident[:])
 
-        point = []
-        for name, src in (("px_rows", px), ("py_rows", py)):
-            rows = keep.tile([P, M_TILES, V], F32, name=name)
-            nc.sync.dma_start(rows[:], src.rearrange("(t p) v -> p t v", p=P))
-            point.append(rows)
-
-        for q in range(QUADRANTS):
-            nc.sync.dma_start(
-                table_scales[32 * q : 32 * q + SCALE_ROWS, :].bitcast(I32),
-                x_scales[0, SCALE_ROWS * q : SCALE_ROWS * (q + 1), :].bitcast(I32),
-            )
+        offsets = keep.tile([P, S // 16], U16)
+        nc.sync.dma_start(offsets[:], offs)
+        px_rows = load_points("px_rows", px)
+        py_rows = load_points("py_rows", py)
+        for r in range(SCALE_ROWS):
+            nc.sync.dma_start(table_scales[r:P:32, :].bitcast(I32), x_scales[0, r : K // 32 : SCALE_ROWS, :].bitcast(I32))
         table_words = keep.tile([P, T], I32)
         nc.sync.dma_start(table_words[:], x_words[0].rearrange("p c r -> p (c r)").bitcast(I32))
-
-        w_raw = []
-        for name, src in (("w1_raw", w1), ("w2_raw", w2)):
-            raw = keep.tile([P, PACK, N], F32, name=name)
-            nc.sync.dma_start(raw[:], src.rearrange("(p j) m -> p j m", j=PACK))
-            w_raw.append(raw)
-
-        def load_bond_row(name, src):
-            cols = keep.tile([P, D], F32, name=name)
-            nc.gpsimd.dma_start(cols[:], src[0].rearrange("(v d) -> v d", d=D))
-            return cols
-
-        bond = [load_bond_row("bx_cols", bx), load_bond_row("by_cols", by)]
+        w1_raw = load_weights("w1_raw", w1)
+        w2_raw = load_weights("w2_raw", w2)
+        bx_cols = load_bond_row("bx_cols", bx)
+        by_cols = load_bond_row("by_cols", by)
         crit_cols = keep.tile([P, M_TILES], F32)
         with nc.allow_non_contiguous_dma(reason="one value a partition"):
-            nc.gpsimd.dma_start(crit_cols[:], crit.rearrange("(t p) o -> p (t o)", p=P))
+            nc.sync.dma_start(crit_cols[:], crit.rearrange("(t p) o -> p (t o)", p=P))
         il_cols = load_bond_row("il_cols", il)
         vol_cols = load_bond_row("vol_cols", vol)
 
+        def group(name, raw, scalar_cols):
+            grouped = keep.tile([P, N, PACK], BF16, name=name, align_bytes=64)
+            dst = grouped[:].rearrange("p (g i) j -> p g j i", i=4)
+            src = raw[:].rearrange("p j (g i) -> p g j i", i=4)
+            cut = scalar_cols // 4
+            nc.scalar.copy(dst[:, :cut], src[:, :cut])
+            if scalar_cols < N:
+                nc.vector.tensor_copy(dst[:, cut:], src[:, cut:])
+            return grouped
+
+        def quantise(name, grouped):
+            codes = keep.tile([P, N], U32, name=name + "_codes", align_bytes=64)
+            scales = keep.tile([P, N], U8, name=name + "_scales", align_bytes=64)
+            nc.vector.quantize_mx(
+                out=codes[:].bitcast(FP8X4), scales=scales[:], in_=grouped[:].rearrange("p m j -> p (m j)")
+            )
+            return codes, scales
+
+        def turn_points(name, rows, b):
+            turned_ps = bank(b, N)
+            for t in range(M_TILES):
+                nc.tensor.transpose(turned_ps[:, t * P : (t + 1) * P], rows[:, t, :], ident[:])
+            turned = keep.tile([P, N], F32, name=name)
+            nc.scalar.copy(turned[:], turned_ps[:])
+            return turned
+
+        px_t = turn_points("px_t", px_rows, 6)
+        py_t = turn_points("py_t", py_rows, 7)
         picked_scales = keep.tile([P, S], U8)
         nc.vector.tensor_copy(picked_scales[:], table_scales[:].indirect(offsets[:]))
         x_scale = keep.tile([P, D, V], U8, align_bytes=64)
@@ -92,62 +117,57 @@ def tile_picked_yperid_dmg_p_kernel(
             x_codes[:].rearrange("p d v -> p v d"), table_words[:].bitcast(U32).indirect(offsets[:])
         )
 
-        point_ps = bank(6, 2 * N)
-        for c in range(2):
-            for t in range(M_TILES):
-                nc.tensor.transpose(point_ps[:, c * N + t * P : c * N + (t + 1) * P], point[c][:, t, :], ident[:])
-        point_t = keep.tile([P, 2 * N], F32)
-        nc.scalar.copy(point_t[:], point_ps[:])
-
-        crit_ps = bank(7, N)
-        for t in range(M_TILES):
-            nc.tensor.transpose(crit_ps[:, t * P : (t + 1) * P], crit_cols[:, t : t + 1].to_broadcast([P, P]), ident[:])
-        crit_t = keep.tile([P, N], F32)
-        nc.scalar.copy(crit_t[:], crit_ps[:])
-
-        squares = []
-        for c in range(2):
-            grouped = keep.tile([P, N, PACK], BF16, name=f"grouped{c}", align_bytes=64)
-            dst = grouped[:].rearrange("p (g i) j -> p g j i", i=4)
-            src = w_raw[c][:].rearrange("p j (g i) -> p g j i", i=4)
-            cut = SCALAR_COLS // 4
-            nc.scalar.copy(dst[:, :cut], src[:, :cut])
-            nc.vector.tensor_copy(dst[:, cut:], src[:, cut:])
-            codes = keep.tile([P, N], U32, name=f"w_codes{c}", align_bytes=64)
-            scales = keep.tile([P, N], U8, name=f"w_scales{c}", align_bytes=64)
-            nc.vector.quantize_mx(
-                out=codes[:].bitcast(FP8X4), scales=scales[:], in_=grouped[:].rearrange("p m j -> p (m j)")
+        def product(w_mx, d, b):
+            acc = bank(b, N)
+            nc.tensor.matmul_mx(
+                out=acc[:],
+                lhsT=x_codes[:, d, :].bitcast(FP8X4),
+                lhsT_scale=x_scale[:, d, :],
+                rhs=w_mx[0][:].bitcast(FP8X4),
+                rhs_scale=w_mx[1][:],
+                start=True,
+                stop=True,
             )
-            diff = keep.tile([P, D, N], F32, name=f"diff{c}")
-            square = keep.tile([P, D, N], F32, name=f"square{c}")
-            for d in range(D):
-                acc = bank(D * c + d, N)
-                nc.tensor.matmul_mx(
-                    out=acc[:],
-                    lhsT=x_codes[:, d, :].bitcast(FP8X4),
-                    lhsT_scale=x_scale[:, d, :],
-                    rhs=codes[:].bitcast(FP8X4),
-                    rhs_scale=scales[:],
-                    start=True,
-                    stop=True,
-                )
-                nc.vector.scalar_tensor_tensor(
-                    diff[:, d, :], acc[:], bond[c][:, d : d + 1], point_t[:, c * N : (c + 1) * N], ALU.add, ALU.subtract
-                )
-                nc.scalar.activation(square[:, d, :], diff[:, d, :], ACT.Square)
-            squares.append(square)
+            return acc
 
+        def bond_square(acc, d, rest, points_t, diff, square):
+            nc.vector.scalar_tensor_tensor(diff[:, d, :], acc[:], rest[:, d : d + 1], points_t[:], ALU.add, ALU.subtract)
+            nc.scalar.activation(square[:, d, :], diff[:, d, :], ACT.Square)
+
+        dx = keep.tile([P, D, N], F32)
+        dx2 = keep.tile([P, D, N], F32)
+        dy = keep.tile([P, D, N], F32)
+        dy2 = keep.tile([P, D, N], F32)
         length2 = keep.tile([P, D, N], F32, tag="staged")
         length = keep.tile([P, D, N], F32)
         margin = keep.tile([P, D, N], F32)
+
+        w1_mx = quantise("w1", group("w1_grouped", w1_raw, W2_SCALAR_COLS))
+        y_ps = [product(w1_mx, d, d) for d in range(D)]
+        w2_grouped = group("w2_grouped", w2_raw, W2_SCALAR_COLS)
+        w2_mx = quantise("w2", w2_grouped)
+        z_ps = [product(w2_mx, d, D + d) for d in range(D)]
         for d in range(D):
-            nc.vector.scalar_tensor_tensor(
-                length2[:, d, :], squares[0][:, d, :], 0.05, squares[1][:, d, :], ALU.add, ALU.add
-            )
+            bond_square(y_ps[d], d, bx_cols, px_t, dx, dx2)
+
+        crit_ps = bank(1, N)
+        for t in range(M_TILES):
+            nc.tensor.transpose(crit_ps[:, t * P : (t + 1) * P], crit_cols[:, t : t + 1].to_broadcast([P, P]), ident[:])
+
+        def bond_length(d):
+            nc.vector.scalar_tensor_tensor(length2[:, d, :], dx2[:, d, :], 0.05, dy2[:, d, :], ALU.add, ALU.add)
             nc.scalar.activation(length[:, d, :], length2[:, d, :], ACT.Sqrt)
+
+        for d in range(D):
+            bond_square(z_ps[d], d, by_cols, py_t, dy, dy2)
+            if d >= 2:
+                bond_length(d - 2)
+        for d in range(D - 2, D):
+            bond_length(d)
+
         for d in range(D):
             nc.vector.scalar_tensor_tensor(
-                margin[:, d, :], length[:, d, :], il_cols[:, d : d + 1], crit_t[:], ALU.mult, ALU.add
+                margin[:, d, :], length[:, d, :], il_cols[:, d : d + 1], crit_ps[:], ALU.mult, ALU.add
             )
 
         vol_sum = keep.tile([P, 1], F32)
@@ -161,13 +181,22 @@ def tile_picked_yperid_dmg_p_kernel(
         weighted = keep.tile([P, D, N], F32)
         for t in range(M_TILES):
             cols = slice(t * P, (t + 1) * P)
-            total = bank(t, V)
+            total = bank(2 + t, V)
             for d in range(D):
                 nc.scalar.activation(intact[:, d, cols], margin[:, d, cols], ACT.Sigmoid, scale=-4.0)
-                nc.vector.tensor_scalar(weighted[:, d, cols], intact[:, d, cols], share[:, d : d + 1], None, ALU.mult)
-                nc.tensor.matmul(
-                    total[:], weighted[:, d, cols], ident[:], start=(d == 0), stop=(d == D - 1), is_transpose=True
-                )
+                if d < 2:
+                    nc.vector.tensor_scalar(weighted[:, d, cols], intact[:, d, cols], share[:, d : d + 1], None, ALU.mult)
+                else:
+                    nc.vector.scalar_tensor_tensor(
+                        weighted[:, d, cols], intact[:, d, cols], share[:, d : d + 1], weighted[:, d - 2, cols], ALU.mult, ALU.add
+                    )
+                    nc.tensor.matmul(
+                        total[:], weighted[:, d, cols], ident[:], start=(d == 2), stop=(d == D - 1), is_transpose=True
+                    )
             result = keep.tile([P, V], F32, name=f"result{t}")
-            nc.vector.tensor_scalar(result[:], total[:], one[:], None, ALU.add)
-            nc.sync.dma_start(out[cols, :], result[:])
+            if t == 0:
+                nc.vector.tensor_scalar(result[:], total[:], one[:], None, ALU.add)
+                nc.sync.dma_start(out[cols, :], result[:])
+            else:
+                nc.scalar.activation(result[:], total[:], ACT.Identity, bias=one[:])
+                nc.scalar.dma_start(out[cols, :], result[:])

from contextlib import ExitStack

import concourse.mybir as mybir
from concourse.masks import make_identity

K, T, S, D, N, V = 512, 2048, 512, 4, 256, 128
P = 128
PACK = 4
M_TILES = N // P
SCALE_ROWS = 4
QUADRANTS = 4

FLOPS = 2 * 2 * K * N * S
BYTES = K * T + (K // 32) * T + 4 * (2 * K * N + 3 * N * V + 4 * S + N) + 2 * P * (S // 16)

F32 = mybir.dt.float32
BF16 = mybir.dt.bfloat16
I32 = mybir.dt.int32
U32 = mybir.dt.uint32
U16 = mybir.dt.uint16
U8 = mybir.dt.uint8
FP8X4 = mybir.dt.float8_e4m3fn_x4
ACT = mybir.ActivationFunctionType
ALU = mybir.AluOpType
AXIS = mybir.AxisListType

W2_SCALAR_COLS = 128


def tile_picked_yperid_dmg_p_kernel(
    tc, x_words, x_scales, w1, w2, px, py, bx, by, il, crit, vol, offs, out
):
    nc = tc.nc
    with ExitStack() as ctx:
        keep = ctx.enter_context(tc.tile_pool(name="keep", bufs=1))
        psum = ctx.enter_context(tc.psum_pool(name="psum", bufs=1))

        def bank(b, cols):
            return psum.tile([P, cols], F32, name=f"bank{b}", tag=f"bank{b}")

        def load_bond_row(name, src):
            cols = keep.tile([P, D], F32, name=name)
            nc.sync.dma_start(cols[:], src[0].rearrange("(v d) -> v d", d=D))
            return cols

        def load_points(name, src):
            rows = keep.tile([P, M_TILES, V], F32, name=name)
            nc.sync.dma_start(rows[:], src.rearrange("(t p) v -> p t v", p=P))
            return rows

        def load_weights(name, src):
            raw = keep.tile([P, PACK, N], F32, name=name)
            nc.sync.dma_start(raw[:], src.rearrange("(p j) m -> p j m", j=PACK))
            return raw

        table_scales = keep.tile([P, T], U8)
        nc.gpsimd.memset(table_scales[:].bitcast(I32), 0)
        one_in = keep.tile([P, 1], F32)
        nc.vector.memset(one_in[:], 1.0)
        one = keep.tile([P, 1], F32)
        nc.scalar.activation(one[:], one_in[:], ACT.Sqrt)
        ident = keep.tile([P, P], F32)
        make_identity(nc, ident[:])

        offsets = keep.tile([P, S // 16], U16)
        nc.sync.dma_start(offsets[:], offs)
        px_rows = load_points("px_rows", px)
        py_rows = load_points("py_rows", py)
        for r in range(SCALE_ROWS):
            nc.sync.dma_start(table_scales[r:P:32, :].bitcast(I32), x_scales[0, r : K // 32 : SCALE_ROWS, :].bitcast(I32))
        table_words = keep.tile([P, T], I32)
        nc.sync.dma_start(table_words[:], x_words[0].rearrange("p c r -> p (c r)").bitcast(I32))
        w1_raw = load_weights("w1_raw", w1)
        w2_raw = load_weights("w2_raw", w2)
        bx_cols = load_bond_row("bx_cols", bx)
        by_cols = load_bond_row("by_cols", by)
        crit_cols = keep.tile([P, M_TILES], F32)
        with nc.allow_non_contiguous_dma(reason="one value a partition"):
            nc.sync.dma_start(crit_cols[:], crit.rearrange("(t p) o -> p (t o)", p=P))
        il_cols = load_bond_row("il_cols", il)
        vol_cols = load_bond_row("vol_cols", vol)

        def group(name, raw, scalar_cols):
            grouped = keep.tile([P, N, PACK], BF16, name=name, align_bytes=64)
            dst = grouped[:].rearrange("p (g i) j -> p g j i", i=4)
            src = raw[:].rearrange("p j (g i) -> p g j i", i=4)
            cut = scalar_cols // 4
            nc.scalar.copy(dst[:, :cut], src[:, :cut])
            if scalar_cols < N:
                nc.vector.tensor_copy(dst[:, cut:], src[:, cut:])
            return grouped

        def quantise(name, grouped):
            codes = keep.tile([P, N], U32, name=name + "_codes", align_bytes=64)
            scales = keep.tile([P, N], U8, name=name + "_scales", align_bytes=64)
            nc.vector.quantize_mx(
                out=codes[:].bitcast(FP8X4), scales=scales[:], in_=grouped[:].rearrange("p m j -> p (m j)")
            )
            return codes, scales

        def turn_points(name, rows, b):
            turned_ps = bank(b, N)
            for t in range(M_TILES):
                nc.tensor.transpose(turned_ps[:, t * P : (t + 1) * P], rows[:, t, :], ident[:])
            turned = keep.tile([P, N], F32, name=name)
            nc.scalar.copy(turned[:], turned_ps[:])
            return turned

        px_t = turn_points("px_t", px_rows, 6)
        py_t = turn_points("py_t", py_rows, 7)
        picked_scales = keep.tile([P, S], U8)
        nc.vector.tensor_copy(picked_scales[:], table_scales[:].indirect(offsets[:]))
        x_scale = keep.tile([P, D, V], U8, align_bytes=64)
        nc.vector.tensor_copy(x_scale[:], picked_scales[:].rearrange("p (v d) -> p d v", d=D))
        x_codes = keep.tile([P, D, V], U32, align_bytes=64)
        nc.vector.tensor_copy(
            x_codes[:].rearrange("p d v -> p v d"), table_words[:].bitcast(U32).indirect(offsets[:])
        )

        def product(w_mx, d, b):
            acc = bank(b, N)
            nc.tensor.matmul_mx(
                out=acc[:],
                lhsT=x_codes[:, d, :].bitcast(FP8X4),
                lhsT_scale=x_scale[:, d, :],
                rhs=w_mx[0][:].bitcast(FP8X4),
                rhs_scale=w_mx[1][:],
                start=True,
                stop=True,
            )
            return acc

        def bond_square(acc, d, rest, points_t, diff, square):
            nc.vector.scalar_tensor_tensor(diff[:, d, :], acc[:], rest[:, d : d + 1], points_t[:], ALU.add, ALU.subtract)
            nc.scalar.activation(square[:, d, :], diff[:, d, :], ACT.Square)

        dx = keep.tile([P, D, N], F32)
        dx2 = keep.tile([P, D, N], F32)
        dy = keep.tile([P, D, N], F32)
        dy2 = keep.tile([P, D, N], F32)
        length2 = keep.tile([P, D, N], F32, tag="staged")
        length = keep.tile([P, D, N], F32)
        margin = keep.tile([P, D, N], F32)

        w1_mx = quantise("w1", group("w1_grouped", w1_raw, W2_SCALAR_COLS))
        y_ps = [product(w1_mx, d, d) for d in range(D)]
        w2_grouped = group("w2_grouped", w2_raw, W2_SCALAR_COLS)
        w2_mx = quantise("w2", w2_grouped)
        z_ps = [product(w2_mx, d, D + d) for d in range(D)]
        for d in range(D):
            bond_square(y_ps[d], d, bx_cols, px_t, dx, dx2)

        crit_ps = bank(1, N)
        for t in range(M_TILES):
            nc.tensor.transpose(crit_ps[:, t * P : (t + 1) * P], crit_cols[:, t : t + 1].to_broadcast([P, P]), ident[:])

        def bond_length(d):
            nc.vector.scalar_tensor_tensor(length2[:, d, :], dx2[:, d, :], 0.05, dy2[:, d, :], ALU.add, ALU.add)
            nc.scalar.activation(length[:, d, :], length2[:, d, :], ACT.Sqrt)

        for d in range(D):
            bond_square(z_ps[d], d, by_cols, py_t, dy, dy2)
            if d >= 2:
                bond_length(d - 2)
        for d in range(D - 2, D):
            bond_length(d)

        for d in range(D):
            nc.vector.scalar_tensor_tensor(
                margin[:, d, :], length[:, d, :], il_cols[:, d : d + 1], crit_ps[:], ALU.mult, ALU.add
            )

        vol_sum = keep.tile([P, 1], F32)
        nc.vector.tensor_reduce(vol_sum[:], vol_cols[:], AXIS.X, ALU.add)
        vol_inv = keep.tile([P, 1], F32)
        nc.vector.reciprocal(vol_inv[:], vol_sum[:])
        share = keep.tile([P, D], F32)
        nc.vector.tensor_scalar(share[:], vol_cols[:], vol_inv[:], -1.0, ALU.mult, ALU.mult)

        intact = keep.tile([P, D, N], F32, tag="staged")
        weighted = keep.tile([P, D, N], F32)
        for t in range(M_TILES):
            cols = slice(t * P, (t + 1) * P)
            total = bank(2 + t, V)
            for d in range(D):
                nc.scalar.activation(intact[:, d, cols], margin[:, d, cols], ACT.Sigmoid, scale=-4.0)
                if d < 2:
                    nc.vector.tensor_scalar(weighted[:, d, cols], intact[:, d, cols], share[:, d : d + 1], None, ALU.mult)
                else:
                    nc.vector.scalar_tensor_tensor(
                        weighted[:, d, cols], intact[:, d, cols], share[:, d : d + 1], weighted[:, d - 2, cols], ALU.mult, ALU.add
                    )
                    nc.tensor.matmul(
                        total[:], weighted[:, d, cols], ident[:], start=(d == 2), stop=(d == D - 1), is_transpose=True
                    )
            result = keep.tile([P, V], F32, name=f"result{t}")
            if t == 0:
                nc.vector.tensor_scalar(result[:], total[:], one[:], None, ALU.add)
                nc.sync.dma_start(out[cols, :], result[:])
            else:
                nc.scalar.activation(result[:], total[:], ACT.Identity, bias=one[:])
                nc.scalar.dma_start(out[cols, :], result[:])
